import numpy as np
import ml_dtypes


def mxq(x, axis, fmt="e4m3"):
    dtype, down = {"e4m3": (ml_dtypes.float8_e4m3fn, 7), "e5m2": (ml_dtypes.float8_e5m2, 14)}[fmt]
    v = np.moveaxis(np.asarray(x, np.float32).astype(ml_dtypes.bfloat16).astype(np.float64), axis, -1)
    blocks = v.reshape(v.shape[:-1] + (-1, 32))
    amax = np.abs(blocks).max(-1, keepdims=True)
    byte = np.maximum(np.where(amax > 0, np.frexp(amax)[1] - 1 + 127, 0) - down, 1)
    scale = np.exp2(byte - 127.0)
    codes = (blocks / scale).astype(np.float32).astype(dtype).astype(np.float64)
    return np.moveaxis((codes * scale).reshape(v.shape), -1, axis)


WIDE = False


def mx_kscale(k):
    if not WIDE:
        return np.ones(k)
    levels = np.array([30, -30])
    if k % 512:
        return np.exp2(np.random.permutation(np.resize(levels, k // 32))).repeat(32)
    a = np.empty((k // 512, 16))
    for p in range(k // 512):
        a[p, :8] = np.random.permutation(np.resize(levels, 8))
        for g in range(8):
            far = levels[np.abs(levels - a[p, g]) >= 10]
            a[p, g + 8] = far[np.random.randint(len(far))]
    return np.exp2(a.ravel()).repeat(32)


def f64(x):
    return np.asarray(x).astype(np.float64)


def striped(idx):
    return np.tile(np.asarray(idx).reshape(-1, 16).T, (8, 1)).astype(np.uint16)


def unstriped(offs):
    return offs[:16].T.reshape(-1).astype(np.int64)


E2M1 = np.array([0.0, 0.5, 1.0, 1.5, 2.0, 3.0, 4.0, 6.0, -0.0, -0.5, -1.0, -1.5, -2.0, -3.0, -4.0, -6.0])


def pack_weight(w, fmt):
    k, n = w.shape
    w = f64(np.asarray(w, np.float32).astype(ml_dtypes.bfloat16)).reshape(k // 32, 32, n)
    amax = np.abs(w).max(1)
    if fmt in ("e4m3", "e5m2"):
        byte = np.frexp(amax)[1] - 1 + 127 - (7 if fmt == "e4m3" else 14)
    else:
        mant, ex = np.frexp(amax / 6.0)
        byte = np.where(mant > 0.5, ex, ex - 1) + 127
    byte = np.clip(np.where(amax > 0, byte, 1), 1, 254)
    scaled = (w * np.exp2(127.0 - byte)[:, None, :]).reshape(k, n).astype(np.float32)
    by_word = np.ascontiguousarray(scaled.reshape(k // 512, 128, 4, n).transpose(0, 1, 3, 2))
    if fmt in ("e4m3", "e5m2"):
        words = by_word.astype(ml_dtypes.float8_e4m3fn if fmt == "e4m3" else ml_dtypes.float8_e5m2).view(np.uint8)
    else:
        c = by_word.astype(ml_dtypes.float4_e2m1fn).view(np.uint8) & 0xF
        words = (c[..., 0::2] | (c[..., 1::2] << 4)).reshape(k // 512, 128, 2 * n)
    return np.ascontiguousarray(words), np.ascontiguousarray(byte.astype(np.uint8).reshape(k // 512, 16, n))


def unpack_weight(words, scales, fmt):
    g, _, n = scales.shape
    words = np.ascontiguousarray(words).reshape(g, 128, n, -1)
    if fmt in ("e4m3", "e5m2"):
        vals = words.view(ml_dtypes.float8_e4m3fn if fmt == "e4m3" else ml_dtypes.float8_e5m2).astype(np.float64)
    else:
        nib = np.empty((g, 128, n, 4), np.uint8)
        nib[..., 0::2] = words & 0xF
        nib[..., 1::2] = words >> 4
        vals = E2M1[nib]
    vals = vals * np.repeat(np.exp2(scales.astype(np.float64) - 127.0), 8, axis=1)[..., None]
    return vals.transpose(0, 1, 3, 2).reshape(g * 512, n)


def bf(x):
    return np.asarray(x, np.float32).astype(ml_dtypes.bfloat16)


def planes(Y):
    r, m = Y.shape
    b = f64(bf(Y)).reshape(r // 32, 32, m)
    amax = np.abs(b).max(1)
    byte = np.clip(np.where(amax > 0, np.frexp(amax)[1] - 1 + 127 - 7, 1), 1, 254)
    codes = (b * np.exp2(127.0 - byte)[:, None, :]).reshape(r, m).astype(np.float32).astype(ml_dtypes.float8_e4m3fn).view(np.uint8)
    words = codes.reshape(r // 512, 128, 4, m).transpose(0, 1, 3, 2)
    return np.ascontiguousarray(words), np.ascontiguousarray(byte.astype(np.uint8).reshape(r // 512, 16, m))


K, T, J, R, C, O, N = 1024, 1024, 256, 512, 1024, 256, 512


def setup_inputs():
    n = np.random.standard_normal
    idx = np.random.permutation(T)[:J]
    idx2 = np.random.permutation(T)[:J]
    idx3 = np.random.permutation(C)[:J]
    idx4 = np.random.permutation(C)[:O]
    fk = mx_kscale(K)
    fr = mx_kscale(R)
    wp = pack_weight(n((K, R)) * 1 / np.sqrt(K) * fk[:, None] * fr, "e5m2")
    wbp = pack_weight(n((R, N)) * np.random.uniform(0.3, 1.7, (1, N)) / np.sqrt(R) / fr[:, None], "e2m1")
    return {
        "xf": (n((K, T))).astype(np.float32),
        "fk": (np.random.uniform(0.5, 2.0, (K, 1)) / fk[:, None]).astype(np.float32),
        "w_words": wp[0],
        "w_scales": wp[1],
        "oldh": (n((R, C)) * 0.7 * fr[:, None]).astype(np.float32),
        "wb_words": wbp[0],
        "wb_scales": wbp[1],
        "rs": (0.6 * n((N, O)) * np.random.uniform(0.2, 2.5, (N, 1)) + np.random.uniform(-1.0, 1.0, (N, 1))).astype(np.float32),
        "offs": striped(idx),
        "offs2": striped(idx2),
        "offs3": striped(idx3),
        "offs4": striped(idx4),
    }


def reference(xf, fk, w_words, w_scales, oldh, wb_words, wb_scales, rs, offs, offs2, offs3, offs4):
    idx = unstriped(offs)
    idx2 = unstriped(offs2)
    idx3 = unstriped(offs3)
    idx4 = unstriped(offs4)
    wu = unpack_weight(w_words, w_scales, "e5m2")
    wbu = unpack_weight(wb_words, wb_scales, "e2m1")
    u = (f64(xf)[:, idx] - f64(xf)[:, idx2]) * f64(fk)
    uq = mxq(u, 0, "e5m2")
    a = wu.T @ uq
    ha = np.maximum(a, 0.0)
    pw0 = np.zeros((R, C))
    pw0[:, idx3] = ha
    pg = pw0 + f64(oldh)
    hid = pg[:, idx4]
    hidq = mxq(hid, 0, "e5m2")
    p = wbu.T @ hidq
    pb = p + f64(rs)
    mn = np.mean(pb, axis=1, keepdims=True)
    d = pb - mn
    y = d / np.sqrt(np.mean(np.square(d), axis=1, keepdims=True) + 0.1)
    words, scales = planes(y)
    return y, words, scales

@@ -1,0 +1,279 @@
+from contextlib import ExitStack
+
+import concourse.mybir as mybir
+
+K, T, J, R, C, O, N = 1024, 1024, 256, 512, 1024, 256, 512
+FLOPS = 2 * K * R * J + 2 * R * N * O
+
+F32 = mybir.dt.float32
+BF16 = mybir.dt.bfloat16
+I32 = mybir.dt.int32
+U32 = mybir.dt.uint32
+U16 = mybir.dt.uint16
+U8 = mybir.dt.uint8
+E5M2X4 = mybir.dt.float8_e5m2_x4
+E4M3X4 = mybir.dt.float8_e4m3fn_x4
+E2M1X4 = mybir.dt.float4_e2m1fn_x4
+ALU = mybir.AluOpType
+ACT = mybir.ActivationFunctionType
+
+P = 128
+PACK = 4
+PASSES = K // (P * PACK)
+SCALAR_PLANES = (0, 1, 4)
+HALF = J // 2
+EPS = 0.1
+
+
+def interleave(nc, grouped, planes):
+    nc.vector.tensor_copy(
+        out=grouped.rearrange("p (c i) t -> p c t i", i=4),
+        in_=planes.rearrange("p t (c i) -> p c t i", i=4),
+    )
+
+
+def tile_list_page_pickgaps_levelled_pl_kernel(
+    tc, xf, fk, w_words, w_scales, oldh, wb_words, wb_scales, rs, offs, offs2, offs3, offs4, out_0, out_1, out_2
+):
+    nc = tc.nc
+    with ExitStack() as ctx:
+        keep = ctx.enter_context(tc.tile_pool(name="keep", bufs=1))
+        psum = ctx.enter_context(tc.psum_pool(name="psum", bufs=1))
+
+        def tile(shape, dtype, name):
+            return keep.tile(shape, dtype, name=name, align_bytes=64)
+
+        list1 = tile([P, J // 16], U16, "list1")
+        list2 = tile([P, J // 16], U16, "list2")
+        list3 = tile([P, J // 16], U16, "list3")
+        list4 = tile([P, O // 16], U16, "list4")
+        x = [tile([P, T], F32, f"x{i}") for i in range(PASSES * PACK)]
+        fk_sb = tile([P, PASSES, PACK], F32, "fk_sb")
+        w_raw = tile([P, PASSES, R], I32, "w_raw")
+        ws_raw = tile([P, PASSES, R], U8, "ws_raw")
+        wb_raw = tile([P, N], U16, "wb_raw")
+        wbs_raw = tile([P, N], U8, "wbs_raw")
+        old = [tile([P, C], F32, f"old{t}") for t in range(PACK)]
+        rs_sb = tile([P, PACK, O], F32, "rs_sb")
+        page = [tile([P, C], F32, f"page{t}") for t in range(PACK)]
+
+        nc.gpsimd.memset(ws_raw[:].rearrange("p z c -> p (z c)").bitcast(U32), 0)
+        nc.gpsimd.memset(wbs_raw[:].bitcast(U32), 0)
+        for t in range(PACK):
+            nc.vector.memset(page[t][:].bitcast(U32), 0)
+
+
+        x_rows = xf.rearrange("(z p t) c -> z t p c", p=P, t=PACK)
+        old_rows = oldh.rearrange("(p t) c -> t p c", t=PACK)
+
+        def load_x(i):
+            nc.sync.dma_start(out=x[i][:], in_=x_rows[i // PACK, i % PACK])
+
+        ws_rows = w_scales.rearrange("z q c -> q z c").bitcast(I32)
+        wbs_rows = wb_scales[0].bitcast(I32)
+
+        def load_ws(q):
+            nc.sync.dma_start(out=ws_raw[32 * q : 32 * q + 4].bitcast(I32), in_=ws_rows[4 * q : 4 * q + 4])
+
+        def load_wbs(q):
+            nc.sync.dma_start(out=wbs_raw[32 * q : 32 * q + 4].bitcast(I32), in_=wbs_rows[4 * q : 4 * q + 4])
+
+        nc.sync.dma_start(list2[:], offs2)
+        nc.sync.dma_start(list1[:], offs)
+        nc.sync.dma_start(out=wb_raw[:].bitcast(I32), in_=wb_words[0].bitcast(I32))
+        load_x(0)
+        nc.sync.dma_start(out=w_raw[:], in_=w_words.rearrange("z p n t -> p z (n t)").bitcast(I32))
+        load_ws(0)
+        load_ws(1)
+        load_x(1)
+        load_ws(2)
+        load_ws(3)
+        nc.sync.dma_start(out=fk_sb[:], in_=fk.rearrange("(z p t) o -> p z (t o)", p=P, t=PACK))
+        load_x(2)
+        load_x(3)
+        load_wbs(0)
+        load_wbs(1)
+        load_x(4)
+        load_wbs(2)
+        load_wbs(3)
+        load_x(5)
+        load_x(6)
+        load_x(7)
+        nc.sync.dma_start(list3[:], offs3)
+        nc.sync.dma_start(list4[:], offs4)
+        for t in (3, 0, 1, 2):
+            nc.sync.dma_start(out=old[t][:], in_=old_rows[t])
+        nc.sync.dma_start(out=rs_sb[:], in_=rs.rearrange("(p t) o -> p t o", t=PACK))
+
+        w_dealt = tile([P, PASSES, PACK, P], I32, "w_dealt")
+        ws_dealt = tile([P, PASSES, PACK, P], U8, "ws_dealt")
+        wb_dealt = tile([P, PACK, P], U16, "wb_dealt")
+
+        def deal_wb():
+            nc.vector.tensor_copy(
+                out=wb_dealt[:].rearrange("p t m -> p m t"),
+                in_=wb_raw[:].rearrange("p (m t) -> p m t", t=PACK),
+            )
+
+        def deal_w():
+            nc.vector.tensor_copy(
+                out=w_dealt[:].rearrange("p z t m -> p z m t"),
+                in_=w_raw[:].rearrange("p z (m t) -> p z m t", t=PACK),
+            )
+
+        def deal_ws():
+            nc.vector.tensor_copy(
+                out=ws_dealt[:].rearrange("p z t m -> p z m t"),
+                in_=ws_raw[:].rearrange("p z (m t) -> p z m t", t=PACK),
+            )
+
+        deal_wb()
+        deals = {0: deal_w, 1: deal_ws}
+
+        acc = [psum.tile([P, J], F32, name=f"acc{t}") for t in range(PACK)]
+        slice_order = (0, 3, 1, 2)
+
+        def quantize(codes, scales, grouped, fmt):
+            nc.vector.quantize_mx(out=codes.bitcast(fmt), scales=scales, in_=grouped.rearrange("p j t -> p (j t)"))
+
+        def gaps(i, gap, cols):
+            n = 16 * (cols.stop - cols.start)
+            second = tile([P, n], F32, f"second{i}_{cols.start}")
+            nc.scalar.activation(second[:], x[i][:].indirect(list2[:, cols]), ACT.Copy)
+            if i in SCALAR_PLANES:
+                first = tile([P, n], F32, f"first{i}")
+                nc.scalar.activation(first[:], x[i][:].indirect(list1[:, cols]), ACT.Copy)
+                nc.vector.tensor_tensor(gap, first[:], second[:], ALU.subtract)
+            else:
+                nc.vector.tensor_tensor(gap, x[i][:].indirect(list1[:, cols]), second[:], ALU.subtract)
+
+        def first_product(z, codes, scales):
+            for t in slice_order:
+                nc.tensor.matmul_mx(
+                    out=acc[t][:],
+                    lhsT=w_dealt[:, z, t, :].bitcast(E5M2X4),
+                    lhsT_scale=ws_dealt[:, z, t, :],
+                    rhs=codes[:].bitcast(E5M2X4),
+                    rhs_scale=scales[:],
+                    start=(z == 0),
+                    stop=(z == PASSES - 1),
+                )
+
+        whole = slice(0, J // 16)
+        halves = [slice(0, J // 32), slice(J // 32, J // 16)]
+        cols = [slice(0, HALF), slice(HALF, J)]
+
+        def scale_and_group(grouped, gap, z):
+            n = grouped.shape[1]
+            nc.vector.tensor_tensor(
+                grouped.rearrange("p (c i) t -> p c t i", i=4),
+                gap.rearrange("p t (c i) -> p c t i", i=4),
+                fk_sb[:, z, :].unsqueeze(1).unsqueeze(3).broadcast_to([P, n // 4, PACK, 4]),
+                ALU.mult,
+            )
+
+        gap0 = tile([P, PACK, J], F32, "gap0")
+        for t in range(PACK):
+            gaps(t, gap0[:, t, :], whole)
+            if t in deals:
+                deals[t]()
+        u0 = tile([P, J, PACK], BF16, "u0")
+        scale_and_group(u0[:], gap0[:], 0)
+        u0_codes = tile([P, J], U32, "u0_codes")
+        u0_scales = tile([P, J], U8, "u0_scales")
+        quantize(u0_codes[:], u0_scales[:], u0[:], E5M2X4)
+        first_product(0, u0_codes, u0_scales)
+
+        gap1 = tile([P, PACK, J], F32, "gap1")
+        for t in range(PACK - 1):
+            gaps(PACK + t, gap1[:, t, :], whole)
+        u1 = [tile([P, HALF, PACK], BF16, f"u1_{h}") for h in range(2)]
+        u1_codes = tile([P, J], U32, "u1_codes")
+        u1_scales = tile([P, J], U8, "u1_scales")
+        for h in range(2):
+            gaps(2 * PACK - 1, gap1[:, PACK - 1, cols[h]], halves[h])
+        for h in range(2):
+            scale_and_group(u1[h][:], gap1[:, :, cols[h]], 1)
+        for h in range(2):
+            quantize(u1_codes[:, cols[h]], u1_scales[:, cols[h]], u1[h][:], E5M2X4)
+        first_product(1, u1_codes, u1_scales)
+        wbs_dealt = keep.tile([P, PACK, P], U8, name="wbs_dealt", tag="u1_1", align_bytes=64)
+        nc.vector.tensor_copy(
+            out=wbs_dealt[:].rearrange("p t m -> p m t"),
+            in_=wbs_raw[:].rearrange("p (m t) -> p m t", t=PACK),
+        )
+
+        ha = [tile([P, J], F32, f"ha{t}") for t in range(PACK)]
+        pg = [tile([P, C], F32, f"pg{t}") for t in range(PACK)]
+        hid_planes = tile([P, PACK, O], BF16, "hid_planes")
+        nc.scalar.activation(ha[0][:], acc[0][:], ACT.Relu)
+        nc.vector.tensor_scalar(ha[3][:], acc[3][:], 0.0, None, ALU.max)
+        nc.scalar.activation(page[0][:].indirect(list3[:]), ha[0][:], ACT.Copy)
+        nc.vector.tensor_copy(page[3][:].indirect(list3[:]), ha[3][:])
+        nc.scalar.activation(ha[1][:], acc[1][:], ACT.Relu)
+        nc.vector.tensor_scalar(ha[2][:], acc[2][:], 0.0, None, ALU.max)
+        nc.scalar.activation(page[1][:].indirect(list3[:]), ha[1][:], ACT.Copy)
+        nc.scalar.activation(page[2][:].indirect(list3[:]), ha[2][:], ACT.Copy)
+        for t in (3, 0, 1, 2):
+            nc.vector.tensor_tensor(pg[t][:], page[t][:], old[t][:], ALU.add)
+        for t in (3, 0, 1):
+            nc.scalar.activation(hid_planes[:, t, :], pg[t][:].indirect(list4[:]), ACT.Copy)
+        nc.vector.tensor_copy(hid_planes[:, 2, :], pg[2][:].indirect(list4[:]))
+
+        hid = [tile([P, HALF, PACK], BF16, f"hid{h}") for h in range(2)]
+        hid_codes = tile([P, O], U32, "hid_codes")
+        hid_scales = tile([P, O], U8, "hid_scales")
+        for h in range(2):
+            interleave(nc, hid[h][:], hid_planes[:, :, cols[h]])
+        for h in range(2):
+            quantize(hid_codes[:, cols[h]], hid_scales[:, cols[h]], hid[h][:], E5M2X4)
+
+        pb = tile([P, PACK, O], F32, "pb")
+        squares = tile([P, PACK, O], F32, "squares")
+        total = tile([P, PACK], F32, "total")
+        sumsq = tile([P, PACK], F32, "sumsq")
+        mean = tile([P, PACK], F32, "mean")
+        inv = tile([P, PACK], F32, "inv")
+        y = tile([P, PACK, O], F32, "y")
+        for t in range(PACK):
+            prod = psum.tile([P, O], F32, name=f"prod{t}")
+            nc.tensor.matmul_mx(
+                out=prod[:],
+                lhsT=wb_dealt[:, t, :].bitcast(E2M1X4),
+                lhsT_scale=wbs_dealt[:, t, :],
+                rhs=hid_codes[:].bitcast(E5M2X4),
+                rhs_scale=hid_scales[:],
+                start=True,
+                stop=True,
+            )
+            nc.vector.scalar_tensor_tensor(
+                pb[:, t, :], prod[:], 1.0, rs_sb[:, t, :], ALU.mult, ALU.add, accum_out=total[:, t : t + 1]
+            )
+            nc.scalar.activation(
+                squares[:, t, :], pb[:, t, :], ACT.Square, bias=total[:, t : t + 1], scale=-float(O),
+                accum_out=sumsq[:, t : t + 1],
+            )
+            if t % 2 == 1:
+                nc.scalar.activation(
+                    inv[:, t - 1 : t + 1], sumsq[:, t - 1 : t + 1], ACT.Abs_reciprocal_sqrt, bias=EPS, scale=1.0 / O**3
+                )
+        nc.vector.tensor_scalar(mean[:], total[:], 1.0 / O, None, ALU.mult)
+        y_rows = out_0.rearrange("(p t) o -> p t o", t=PACK)
+        for t in range(PACK):
+            nc.vector.tensor_scalar(
+                y[:, t, :], pb[:, t, :], mean[:, t : t + 1], inv[:, t : t + 1], ALU.subtract, ALU.mult
+            )
+            if t % 2 == 1:
+                nc.sync.dma_start(out=y_rows[:, t - 1 : t + 1, :], in_=y[:, t - 1 : t + 1, :])
+        y_bf = [tile([P, HALF, PACK], BF16, f"y_bf{h}") for h in range(2)]
+        y_codes = tile([P, O], U32, "y_codes")
+        y_scales = tile([P, O], U8, "y_scales")
+        for h in range(2):
+            interleave(nc, y_bf[h][:], y[:, :, cols[h]])
+        for h in range(2):
+            quantize(y_codes[:, cols[h]], y_scales[:, cols[h]], y_bf[h][:], E4M3X4)
+        nc.scalar.dma_start(out=out_1[0].rearrange("p c t -> p (c t)").bitcast(I32), in_=y_codes[:].bitcast(I32))
+        scale_rows = out_2[0].bitcast(I32)
+        for q in range(4):
+            queue = nc.scalar if q == 3 else nc.sync
+            queue.dma_start(out=scale_rows[4 * q : 4 * q + 4], in_=y_scales[32 * q : 32 * q + 4].bitcast(I32))

@@ -49,7 +49,7 @@ def tile_list_page_pickgaps_levelled_pl_kernel(
         list4 = tile([P, O // 16], U16, "list4")
         x = [tile([P, T], F32, f"x{i}") for i in range(PASSES * PACK)]
         fk_sb = tile([P, PASSES, PACK], F32, "fk_sb")
-        w_raw = tile([P, PASSES, R], I32, "w_raw")
+        w_raw = [tile([P, R], I32, f"w_raw{z}") for z in range(PASSES)]
         ws_raw = tile([P, PASSES, R], U8, "ws_raw")
         wb_raw = tile([P, N], U16, "wb_raw")
         wbs_raw = tile([P, N], U8, "wbs_raw")
@@ -62,6 +62,9 @@ def tile_list_page_pickgaps_levelled_pl_kernel(
         for t in range(PACK):
             nc.vector.memset(page[t][:].bitcast(U32), 0)
 
+        warm = tile([P, 2], F32, "warm")
+        nc.gpsimd.memset(warm[:], 1.0)
+        nc.scalar.activation(warm[:, 1:2], warm[:, 0:1], ACT.Abs_reciprocal_sqrt)
 
         x_rows = xf.rearrange("(z p t) c -> z t p c", p=P, t=PACK)
         old_rows = oldh.rearrange("(p t) c -> t p c", t=PACK)
@@ -72,6 +75,9 @@ def tile_list_page_pickgaps_levelled_pl_kernel(
         ws_rows = w_scales.rearrange("z q c -> q z c").bitcast(I32)
         wbs_rows = wb_scales[0].bitcast(I32)
 
+        def load_w(z):
+            nc.sync.dma_start(out=w_raw[z][:], in_=w_words[z].rearrange("p n t -> p (n t)").bitcast(I32))
+
         def load_ws(q):
             nc.sync.dma_start(out=ws_raw[32 * q : 32 * q + 4].bitcast(I32), in_=ws_rows[4 * q : 4 * q + 4])
 
@@ -80,45 +86,33 @@ def tile_list_page_pickgaps_levelled_pl_kernel(
 
         nc.sync.dma_start(list2[:], offs2)
         nc.sync.dma_start(list1[:], offs)
-        nc.sync.dma_start(out=wb_raw[:].bitcast(I32), in_=wb_words[0].bitcast(I32))
+        for q in range(4):
+            load_ws(q)
         load_x(0)
-        nc.sync.dma_start(out=w_raw[:], in_=w_words.rearrange("z p n t -> p z (n t)").bitcast(I32))
-        load_ws(0)
-        load_ws(1)
+        load_w(0)
         load_x(1)
-        load_ws(2)
-        load_ws(3)
         nc.sync.dma_start(out=fk_sb[:], in_=fk.rearrange("(z p t) o -> p z (t o)", p=P, t=PACK))
-        load_x(2)
-        load_x(3)
-        load_wbs(0)
-        load_wbs(1)
-        load_x(4)
-        load_wbs(2)
-        load_wbs(3)
-        load_x(5)
-        load_x(6)
-        load_x(7)
+        for i in range(2, PASSES * PACK):
+            load_x(i)
+        load_w(1)
+        nc.sync.dma_start(out=wb_raw[:].bitcast(I32), in_=wb_words[0].bitcast(I32))
+        for q in range(4):
+            load_wbs(q)
         nc.sync.dma_start(list3[:], offs3)
+        nc.sync.dma_start(out=old[0][:], in_=old_rows[0])
+        nc.sync.dma_start(out=old[3][:], in_=old_rows[3])
         nc.sync.dma_start(list4[:], offs4)
-        for t in (3, 0, 1, 2):
-            nc.sync.dma_start(out=old[t][:], in_=old_rows[t])
+        nc.sync.dma_start(out=old[1][:], in_=old_rows[1])
+        nc.sync.dma_start(out=old[2][:], in_=old_rows[2])
         nc.sync.dma_start(out=rs_sb[:], in_=rs.rearrange("(p t) o -> p t o", t=PACK))
 
-        w_dealt = tile([P, PASSES, PACK, P], I32, "w_dealt")
+        w_dealt = [tile([P, PACK, P], I32, f"w_dealt{z}") for z in range(PASSES)]
         ws_dealt = tile([P, PASSES, PACK, P], U8, "ws_dealt")
-        wb_dealt = tile([P, PACK, P], U16, "wb_dealt")
 
-        def deal_wb():
+        def deal_w(z):
             nc.vector.tensor_copy(
-                out=wb_dealt[:].rearrange("p t m -> p m t"),
-                in_=wb_raw[:].rearrange("p (m t) -> p m t", t=PACK),
-            )
-
-        def deal_w():
-            nc.vector.tensor_copy(
-                out=w_dealt[:].rearrange("p z t m -> p z m t"),
-                in_=w_raw[:].rearrange("p z (m t) -> p z m t", t=PACK),
+                out=w_dealt[z][:].rearrange("p t m -> p m t"),
+                in_=w_raw[z][:].rearrange("p (m t) -> p m t", t=PACK),
             )
 
         def deal_ws():
@@ -127,11 +121,10 @@ def tile_list_page_pickgaps_levelled_pl_kernel(
                 in_=ws_raw[:].rearrange("p z (m t) -> p z m t", t=PACK),
             )
 
-        deal_wb()
-        deals = {0: deal_w, 1: deal_ws}
+        deal_ws()
 
         acc = [psum.tile([P, J], F32, name=f"acc{t}") for t in range(PACK)]
-        slice_order = (0, 3, 1, 2)
+        slice_order = (0, 1, 3, 2)
 
         def quantize(codes, scales, grouped, fmt):
             nc.vector.quantize_mx(out=codes.bitcast(fmt), scales=scales, in_=grouped.rearrange("p j t -> p (j t)"))
@@ -151,7 +144,7 @@ def tile_list_page_pickgaps_levelled_pl_kernel(
             for t in slice_order:
                 nc.tensor.matmul_mx(
                     out=acc[t][:],
-                    lhsT=w_dealt[:, z, t, :].bitcast(E5M2X4),
+                    lhsT=w_dealt[z][:, t, :].bitcast(E5M2X4),
                     lhsT_scale=ws_dealt[:, z, t, :],
                     rhs=codes[:].bitcast(E5M2X4),
                     rhs_scale=scales[:],
@@ -175,8 +168,8 @@ def tile_list_page_pickgaps_levelled_pl_kernel(
         gap0 = tile([P, PACK, J], F32, "gap0")
         for t in range(PACK):
             gaps(t, gap0[:, t, :], whole)
-            if t in deals:
-                deals[t]()
+            if t == 0:
+                deal_w(0)
         u0 = tile([P, J, PACK], BF16, "u0")
         scale_and_group(u0[:], gap0[:], 0)
         u0_codes = tile([P, J], U32, "u0_codes")
@@ -192,11 +185,17 @@ def tile_list_page_pickgaps_levelled_pl_kernel(
         u1_scales = tile([P, J], U8, "u1_scales")
         for h in range(2):
             gaps(2 * PACK - 1, gap1[:, PACK - 1, cols[h]], halves[h])
+        deal_w(1)
         for h in range(2):
             scale_and_group(u1[h][:], gap1[:, :, cols[h]], 1)
         for h in range(2):
             quantize(u1_codes[:, cols[h]], u1_scales[:, cols[h]], u1[h][:], E5M2X4)
         first_product(1, u1_codes, u1_scales)
+        wb_dealt = keep.tile([P, PACK, P], U16, name="wb_dealt", tag="u1_0", align_bytes=64)
+        nc.vector.tensor_copy(
+            out=wb_dealt[:].rearrange("p t m -> p m t"),
+            in_=wb_raw[:].rearrange("p (m t) -> p m t", t=PACK),
+        )
         wbs_dealt = keep.tile([P, PACK, P], U8, name="wbs_dealt", tag="u1_1", align_bytes=64)
         nc.vector.tensor_copy(
             out=wbs_dealt[:].rearrange("p t m -> p m t"),
@@ -206,19 +205,18 @@ def tile_list_page_pickgaps_levelled_pl_kernel(
         ha = [tile([P, J], F32, f"ha{t}") for t in range(PACK)]
         pg = [tile([P, C], F32, f"pg{t}") for t in range(PACK)]
         hid_planes = tile([P, PACK, O], BF16, "hid_planes")
-        nc.scalar.activation(ha[0][:], acc[0][:], ACT.Relu)
-        nc.vector.tensor_scalar(ha[3][:], acc[3][:], 0.0, None, ALU.max)
-        nc.scalar.activation(page[0][:].indirect(list3[:]), ha[0][:], ACT.Copy)
+        for t in (0, 1):
+            nc.scalar.activation(ha[t][:], acc[t][:], ACT.Relu)
+        for t in (3, 2):
+            nc.vector.tensor_scalar(ha[t][:], acc[t][:], 0.0, None, ALU.max)
+        for t in (0, 1, 2):
+            nc.scalar.activation(page[t][:].indirect(list3[:]), ha[t][:], ACT.Copy)
         nc.vector.tensor_copy(page[3][:].indirect(list3[:]), ha[3][:])
-        nc.scalar.activation(ha[1][:], acc[1][:], ACT.Relu)
-        nc.vector.tensor_scalar(ha[2][:], acc[2][:], 0.0, None, ALU.max)
-        nc.scalar.activation(page[1][:].indirect(list3[:]), ha[1][:], ACT.Copy)
-        nc.scalar.activation(page[2][:].indirect(list3[:]), ha[2][:], ACT.Copy)
-        for t in (3, 0, 1, 2):
+        for t in (0, 3, 1, 2):
             nc.vector.tensor_tensor(pg[t][:], page[t][:], old[t][:], ALU.add)
-        for t in (3, 0, 1):
+        for t in (0, 3, 2):
             nc.scalar.activation(hid_planes[:, t, :], pg[t][:].indirect(list4[:]), ACT.Copy)
-        nc.vector.tensor_copy(hid_planes[:, 2, :], pg[2][:].indirect(list4[:]))
+        nc.vector.tensor_copy(hid_planes[:, 1, :], pg[1][:].indirect(list4[:]))
 
         hid = [tile([P, HALF, PACK], BF16, f"hid{h}") for h in range(2)]
         hid_codes = tile([P, O], U32, "hid_codes")
@@ -235,7 +233,9 @@ def tile_list_page_pickgaps_levelled_pl_kernel(
         mean = tile([P, PACK], F32, "mean")
         inv = tile([P, PACK], F32, "inv")
         y = tile([P, PACK, O], F32, "y")
-        for t in range(PACK):
+        y_rows = out_0.rearrange("(p t) o -> p t o", t=PACK)
+
+        def add_residual(t):
             prod = psum.tile([P, O], F32, name=f"prod{t}")
             nc.tensor.matmul_mx(
                 out=prod[:],
@@ -253,18 +253,33 @@ def tile_list_page_pickgaps_levelled_pl_kernel(
                 squares[:, t, :], pb[:, t, :], ACT.Square, bias=total[:, t : t + 1], scale=-float(O),
                 accum_out=sumsq[:, t : t + 1],
             )
-            if t % 2 == 1:
-                nc.scalar.activation(
-                    inv[:, t - 1 : t + 1], sumsq[:, t - 1 : t + 1], ACT.Abs_reciprocal_sqrt, bias=EPS, scale=1.0 / O**3
-                )
-        nc.vector.tensor_scalar(mean[:], total[:], 1.0 / O, None, ALU.mult)
-        y_rows = out_0.rearrange("(p t) o -> p t o", t=PACK)
-        for t in range(PACK):
+
+        def inverse_spread(pair):
+            nc.scalar.activation(inv[:, pair], sumsq[:, pair], ACT.Abs_reciprocal_sqrt, bias=EPS, scale=1.0 / O**3)
+
+        def row_mean(pair):
+            nc.vector.tensor_scalar(mean[:, pair], total[:, pair], 1.0 / O, None, ALU.mult)
+
+        def normalise(t):
             nc.vector.tensor_scalar(
                 y[:, t, :], pb[:, t, :], mean[:, t : t + 1], inv[:, t : t + 1], ALU.subtract, ALU.mult
             )
-            if t % 2 == 1:
-                nc.sync.dma_start(out=y_rows[:, t - 1 : t + 1, :], in_=y[:, t - 1 : t + 1, :])
+
+        low, high = slice(0, 2), slice(2, 4)
+        add_residual(0)
+        add_residual(1)
+        add_residual(2)
+        inverse_spread(low)
+        row_mean(low)
+        add_residual(3)
+        inverse_spread(high)
+        normalise(0)
+        row_mean(high)
+        normalise(1)
+        nc.sync.dma_start(out=y_rows[:, low, :], in_=y[:, low, :])
+        normalise(2)
+        normalise(3)
+        nc.sync.dma_start(out=y_rows[:, high, :], in_=y[:, high, :])
         y_bf = [tile([P, HALF, PACK], BF16, f"y_bf{h}") for h in range(2)]
         y_codes = tile([P, O], U32, "y_codes")
         y_scales = tile([P, O], U8, "y_scales")

@@ -84,16 +84,17 @@ def tile_list_page_pickgaps_levelled_pl_kernel(
         def load_wbs(q):
             nc.sync.dma_start(out=wbs_raw[32 * q : 32 * q + 4].bitcast(I32), in_=wbs_rows[4 * q : 4 * q + 4])
 
+        load_x(0)
         nc.sync.dma_start(list2[:], offs2)
         nc.sync.dma_start(list1[:], offs)
+        load_x(1)
+        load_x(2)
         for q in range(4):
             load_ws(q)
-        load_x(0)
-        load_w(0)
-        load_x(1)
         nc.sync.dma_start(out=fk_sb[:], in_=fk.rearrange("(z p t) o -> p z (t o)", p=P, t=PACK))
-        for i in range(2, PASSES * PACK):
+        for i in range(3, PASSES * PACK):
             load_x(i)
+        load_w(0)
         load_w(1)
         nc.sync.dma_start(out=wb_raw[:].bitcast(I32), in_=wb_words[0].bitcast(I32))
         for q in range(4):
@@ -117,11 +118,9 @@ def tile_list_page_pickgaps_levelled_pl_kernel(
 
         def deal_ws():
             nc.vector.tensor_copy(
-                out=ws_dealt[:].rearrange("p z t m -> p z m t"),
-                in_=ws_raw[:].rearrange("p z (m t) -> p z m t", t=PACK),
+                out=ws_dealt[:], in_=ws_raw[:].rearrange("p z (m t) -> p z t m", t=PACK)
             )
 
-        deal_ws()
 
         acc = [psum.tile([P, J], F32, name=f"acc{t}") for t in range(PACK)]
         slice_order = (0, 1, 3, 2)
@@ -168,14 +167,13 @@ def tile_list_page_pickgaps_levelled_pl_kernel(
         gap0 = tile([P, PACK, J], F32, "gap0")
         for t in range(PACK):
             gaps(t, gap0[:, t, :], whole)
-            if t == 0:
-                deal_w(0)
+            if t == 1:
+                deal_ws()
         u0 = tile([P, J, PACK], BF16, "u0")
         scale_and_group(u0[:], gap0[:], 0)
         u0_codes = tile([P, J], U32, "u0_codes")
         u0_scales = tile([P, J], U8, "u0_scales")
         quantize(u0_codes[:], u0_scales[:], u0[:], E5M2X4)
-        first_product(0, u0_codes, u0_scales)
 
         gap1 = tile([P, PACK, J], F32, "gap1")
         for t in range(PACK - 1):
@@ -185,6 +183,8 @@ def tile_list_page_pickgaps_levelled_pl_kernel(
         u1_scales = tile([P, J], U8, "u1_scales")
         for h in range(2):
             gaps(2 * PACK - 1, gap1[:, PACK - 1, cols[h]], halves[h])
+        deal_w(0)
+        first_product(0, u0_codes, u0_scales)
         deal_w(1)
         for h in range(2):
             scale_and_group(u1[h][:], gap1[:, :, cols[h]], 1)
@@ -193,13 +193,11 @@ def tile_list_page_pickgaps_levelled_pl_kernel(
         first_product(1, u1_codes, u1_scales)
         wb_dealt = keep.tile([P, PACK, P], U16, name="wb_dealt", tag="u1_0", align_bytes=64)
         nc.vector.tensor_copy(
-            out=wb_dealt[:].rearrange("p t m -> p m t"),
-            in_=wb_raw[:].rearrange("p (m t) -> p m t", t=PACK),
+            out=wb_dealt[:], in_=wb_raw[:].rearrange("p (m t) -> p t m", t=PACK)
         )
         wbs_dealt = keep.tile([P, PACK, P], U8, name="wbs_dealt", tag="u1_1", align_bytes=64)
         nc.vector.tensor_copy(
-            out=wbs_dealt[:].rearrange("p t m -> p m t"),
-            in_=wbs_raw[:].rearrange("p (m t) -> p m t", t=PACK),
+            out=wbs_dealt[:], in_=wbs_raw[:].rearrange("p (m t) -> p t m", t=PACK)
         )
 
         ha = [tile([P, J], F32, f"ha{t}") for t in range(PACK)]
@@ -214,9 +212,10 @@ def tile_list_page_pickgaps_levelled_pl_kernel(
         nc.vector.tensor_copy(page[3][:].indirect(list3[:]), ha[3][:])
         for t in (0, 3, 1, 2):
             nc.vector.tensor_tensor(pg[t][:], page[t][:], old[t][:], ALU.add)
-        for t in (0, 3, 2):
+        for t in (0, 3, 1):
             nc.scalar.activation(hid_planes[:, t, :], pg[t][:].indirect(list4[:]), ACT.Copy)
-        nc.vector.tensor_copy(hid_planes[:, 1, :], pg[1][:].indirect(list4[:]))
+        nc.scalar.activation(hid_planes[:, 2, cols[1]], pg[2][:].indirect(list4[:, halves[1]]), ACT.Copy)
+        nc.vector.tensor_copy(hid_planes[:, 2, cols[0]], pg[2][:].indirect(list4[:, halves[0]]))
 
         hid = [tile([P, HALF, PACK], BF16, f"hid{h}") for h in range(2)]
         hid_codes = tile([P, O], U32, "hid_codes")
@@ -232,7 +231,8 @@ def tile_list_page_pickgaps_levelled_pl_kernel(
         sumsq = tile([P, PACK], F32, "sumsq")
         mean = tile([P, PACK], F32, "mean")
         inv = tile([P, PACK], F32, "inv")
-        y = tile([P, PACK, O], F32, "y")
+        y_low = tile([P, 2, O], F32, "y_low")
+        y_high = tile([P, 2, O], F32, "y_high")
         y_rows = out_0.rearrange("(p t) o -> p t o", t=PACK)
 
         def add_residual(t):
@@ -260,11 +260,13 @@ def tile_list_page_pickgaps_levelled_pl_kernel(
         def row_mean(pair):
             nc.vector.tensor_scalar(mean[:, pair], total[:, pair], 1.0 / O, None, ALU.mult)
 
-        def normalise(t):
+        def normalise(t, part):
+            dst = y_low if t < 2 else y_high
             nc.vector.tensor_scalar(
-                y[:, t, :], pb[:, t, :], mean[:, t : t + 1], inv[:, t : t + 1], ALU.subtract, ALU.mult
+                dst[:, t % 2, part], pb[:, t, part], mean[:, t : t + 1], inv[:, t : t + 1], ALU.subtract, ALU.mult
             )
 
+        y_bf = [tile([P, HALF, PACK], BF16, f"y_bf{h}") for h in range(2)]
         low, high = slice(0, 2), slice(2, 4)
         add_residual(0)
         add_residual(1)
@@ -272,22 +274,27 @@ def tile_list_page_pickgaps_levelled_pl_kernel(
         inverse_spread(low)
         row_mean(low)
         add_residual(3)
-        inverse_spread(high)
-        normalise(0)
+        inverse_spread(slice(2, 3))
+        inverse_spread(slice(3, 4))
+        normalise(0, slice(0, O))
         row_mean(high)
-        normalise(1)
-        nc.sync.dma_start(out=y_rows[:, low, :], in_=y[:, low, :])
-        normalise(2)
-        normalise(3)
-        nc.sync.dma_start(out=y_rows[:, high, :], in_=y[:, high, :])
-        y_bf = [tile([P, HALF, PACK], BF16, f"y_bf{h}") for h in range(2)]
+        normalise(1, slice(0, O))
+        nc.sync.dma_start(out=y_rows[:, low, :], in_=y_low[:])
+        for h in range(2):
+            interleave(nc, y_bf[h][:, :, low], y_low[:, :, cols[h]])
+        normalise(2, slice(0, O))
+        normalise(3, cols[0])
+        normalise(3, cols[1])
+        nc.sync.dma_start(out=y_rows[:, high, :], in_=y_high[:])
         y_codes = tile([P, O], U32, "y_codes")
         y_scales = tile([P, O], U8, "y_scales")
         for h in range(2):
-            interleave(nc, y_bf[h][:], y[:, :, cols[h]])
+            interleave(nc, y_bf[h][:, :, high], y_high[:, :, cols[h]])
         for h in range(2):
             quantize(y_codes[:, cols[h]], y_scales[:, cols[h]], y_bf[h][:], E4M3X4)
-        nc.scalar.dma_start(out=out_1[0].rearrange("p c t -> p (c t)").bitcast(I32), in_=y_codes[:].bitcast(I32))
+        word_rows = out_1[0].rearrange("p c t -> p (c t)").bitcast(I32)
+        nc.sync.dma_start(out=word_rows[:, cols[0]], in_=y_codes[:, cols[0]].bitcast(I32))
+        nc.scalar.dma_start(out=word_rows[:, cols[1]], in_=y_codes[:, cols[1]].bitcast(I32))
         scale_rows = out_2[0].bitcast(I32)
         for q in range(4):
             queue = nc.scalar if q == 3 else nc.sync

from contextlib import ExitStack

import concourse.mybir as mybir

K, T, J, R, C, O, N = 1024, 1024, 256, 512, 1024, 256, 512
FLOPS = 2 * K * R * J + 2 * R * N * O

F32 = mybir.dt.float32
BF16 = mybir.dt.bfloat16
I32 = mybir.dt.int32
U32 = mybir.dt.uint32
U16 = mybir.dt.uint16
U8 = mybir.dt.uint8
E5M2X4 = mybir.dt.float8_e5m2_x4
E4M3X4 = mybir.dt.float8_e4m3fn_x4
E2M1X4 = mybir.dt.float4_e2m1fn_x4
ALU = mybir.AluOpType
ACT = mybir.ActivationFunctionType

P = 128
PACK = 4
PASSES = K // (P * PACK)
SCALAR_PLANES = (0, 1, 4)
HALF = J // 2
EPS = 0.1


def interleave(nc, grouped, planes):
    nc.vector.tensor_copy(
        out=grouped.rearrange("p (c i) t -> p c t i", i=4),
        in_=planes.rearrange("p t (c i) -> p c t i", i=4),
    )


def tile_list_page_pickgaps_levelled_pl_kernel(
    tc, xf, fk, w_words, w_scales, oldh, wb_words, wb_scales, rs, offs, offs2, offs3, offs4, out_0, out_1, out_2
):
    nc = tc.nc
    with ExitStack() as ctx:
        keep = ctx.enter_context(tc.tile_pool(name="keep", bufs=1))
        psum = ctx.enter_context(tc.psum_pool(name="psum", bufs=1))

        def tile(shape, dtype, name):
            return keep.tile(shape, dtype, name=name, align_bytes=64)

        list1 = tile([P, J // 16], U16, "list1")
        list2 = tile([P, J // 16], U16, "list2")
        list3 = tile([P, J // 16], U16, "list3")
        list4 = tile([P, O // 16], U16, "list4")
        x = [tile([P, T], F32, f"x{i}") for i in range(PASSES * PACK)]
        fk_sb = tile([P, PASSES, PACK], F32, "fk_sb")
        w_raw = [tile([P, R], I32, f"w_raw{z}") for z in range(PASSES)]
        ws_raw = tile([P, PASSES, R], U8, "ws_raw")
        wb_raw = tile([P, N], U16, "wb_raw")
        wbs_raw = tile([P, N], U8, "wbs_raw")
        old = [tile([P, C], F32, f"old{t}") for t in range(PACK)]
        rs_sb = tile([P, PACK, O], F32, "rs_sb")
        page = [tile([P, C], F32, f"page{t}") for t in range(PACK)]

        nc.gpsimd.memset(ws_raw[:].rearrange("p z c -> p (z c)").bitcast(U32), 0)
        nc.gpsimd.memset(wbs_raw[:].bitcast(U32), 0)
        for t in range(PACK):
            nc.vector.memset(page[t][:].bitcast(U32), 0)

        warm = tile([P, 2], F32, "warm")
        nc.gpsimd.memset(warm[:], 1.0)
        nc.scalar.activation(warm[:, 1:2], warm[:, 0:1], ACT.Abs_reciprocal_sqrt)

        x_rows = xf.rearrange("(z p t) c -> z t p c", p=P, t=PACK)
        old_rows = oldh.rearrange("(p t) c -> t p c", t=PACK)

        def load_x(i):
            nc.sync.dma_start(out=x[i][:], in_=x_rows[i // PACK, i % PACK])

        ws_rows = w_scales.rearrange("z q c -> q z c").bitcast(I32)
        wbs_rows = wb_scales[0].bitcast(I32)

        def load_w(z):
            nc.sync.dma_start(out=w_raw[z][:], in_=w_words[z].rearrange("p n t -> p (n t)").bitcast(I32))

        def load_ws(q):
            nc.sync.dma_start(out=ws_raw[32 * q : 32 * q + 4].bitcast(I32), in_=ws_rows[4 * q : 4 * q + 4])

        def load_wbs(q):
            nc.sync.dma_start(out=wbs_raw[32 * q : 32 * q + 4].bitcast(I32), in_=wbs_rows[4 * q : 4 * q + 4])

        load_x(0)
        nc.sync.dma_start(list2[:], offs2)
        nc.sync.dma_start(list1[:], offs)
        load_x(1)
        load_x(2)
        for q in range(4):
            load_ws(q)
        nc.sync.dma_start(out=fk_sb[:], in_=fk.rearrange("(z p t) o -> p z (t o)", p=P, t=PACK))
        for i in range(3, PASSES * PACK):
            load_x(i)
        load_w(0)
        load_w(1)
        nc.sync.dma_start(out=wb_raw[:].bitcast(I32), in_=wb_words[0].bitcast(I32))
        for q in range(4):
            load_wbs(q)
        nc.sync.dma_start(list3[:], offs3)
        nc.sync.dma_start(out=old[0][:], in_=old_rows[0])
        nc.sync.dma_start(out=old[3][:], in_=old_rows[3])
        nc.sync.dma_start(list4[:], offs4)
        nc.sync.dma_start(out=old[1][:], in_=old_rows[1])
        nc.sync.dma_start(out=old[2][:], in_=old_rows[2])
        nc.sync.dma_start(out=rs_sb[:], in_=rs.rearrange("(p t) o -> p t o", t=PACK))

        w_dealt = [tile([P, PACK, P], I32, f"w_dealt{z}") for z in range(PASSES)]
        ws_dealt = tile([P, PASSES, PACK, P], U8, "ws_dealt")

        def deal_w(z):
            nc.vector.tensor_copy(
                out=w_dealt[z][:].rearrange("p t m -> p m t"),
                in_=w_raw[z][:].rearrange("p (m t) -> p m t", t=PACK),
            )

        def deal_ws():
            nc.vector.tensor_copy(
                out=ws_dealt[:], in_=ws_raw[:].rearrange("p z (m t) -> p z t m", t=PACK)
            )


        acc = [psum.tile([P, J], F32, name=f"acc{t}") for t in range(PACK)]
        slice_order = (0, 1, 3, 2)

        def quantize(codes, scales, grouped, fmt):
            nc.vector.quantize_mx(out=codes.bitcast(fmt), scales=scales, in_=grouped.rearrange("p j t -> p (j t)"))

        def gaps(i, gap, cols):
            n = 16 * (cols.stop - cols.start)
            second = tile([P, n], F32, f"second{i}_{cols.start}")
            nc.scalar.activation(second[:], x[i][:].indirect(list2[:, cols]), ACT.Copy)
            if i in SCALAR_PLANES:
                first = tile([P, n], F32, f"first{i}")
                nc.scalar.activation(first[:], x[i][:].indirect(list1[:, cols]), ACT.Copy)
                nc.vector.tensor_tensor(gap, first[:], second[:], ALU.subtract)
            else:
                nc.vector.tensor_tensor(gap, x[i][:].indirect(list1[:, cols]), second[:], ALU.subtract)

        def first_product(z, codes, scales):
            for t in slice_order:
                nc.tensor.matmul_mx(
                    out=acc[t][:],
                    lhsT=w_dealt[z][:, t, :].bitcast(E5M2X4),
                    lhsT_scale=ws_dealt[:, z, t, :],
                    rhs=codes[:].bitcast(E5M2X4),
                    rhs_scale=scales[:],
                    start=(z == 0),
                    stop=(z == PASSES - 1),
                )

        whole = slice(0, J // 16)
        halves = [slice(0, J // 32), slice(J // 32, J // 16)]
        cols = [slice(0, HALF), slice(HALF, J)]

        def scale_and_group(grouped, gap, z):
            n = grouped.shape[1]
            nc.vector.tensor_tensor(
                grouped.rearrange("p (c i) t -> p c t i", i=4),
                gap.rearrange("p t (c i) -> p c t i", i=4),
                fk_sb[:, z, :].unsqueeze(1).unsqueeze(3).broadcast_to([P, n // 4, PACK, 4]),
                ALU.mult,
            )

        gap0 = tile([P, PACK, J], F32, "gap0")
        for t in range(PACK):
            gaps(t, gap0[:, t, :], whole)
            if t == 1:
                deal_ws()
        u0 = tile([P, J, PACK], BF16, "u0")
        scale_and_group(u0[:], gap0[:], 0)
        u0_codes = tile([P, J], U32, "u0_codes")
        u0_scales = tile([P, J], U8, "u0_scales")
        quantize(u0_codes[:], u0_scales[:], u0[:], E5M2X4)

        gap1 = tile([P, PACK, J], F32, "gap1")
        for t in range(PACK - 1):
            gaps(PACK + t, gap1[:, t, :], whole)
        u1 = [tile([P, HALF, PACK], BF16, f"u1_{h}") for h in range(2)]
        u1_codes = tile([P, J], U32, "u1_codes")
        u1_scales = tile([P, J], U8, "u1_scales")
        for h in range(2):
            gaps(2 * PACK - 1, gap1[:, PACK - 1, cols[h]], halves[h])
        deal_w(0)
        first_product(0, u0_codes, u0_scales)
        deal_w(1)
        for h in range(2):
            scale_and_group(u1[h][:], gap1[:, :, cols[h]], 1)
        for h in range(2):
            quantize(u1_codes[:, cols[h]], u1_scales[:, cols[h]], u1[h][:], E5M2X4)
        first_product(1, u1_codes, u1_scales)
        wb_dealt = keep.tile([P, PACK, P], U16, name="wb_dealt", tag="u1_0", align_bytes=64)
        nc.vector.tensor_copy(
            out=wb_dealt[:], in_=wb_raw[:].rearrange("p (m t) -> p t m", t=PACK)
        )
        wbs_dealt = keep.tile([P, PACK, P], U8, name="wbs_dealt", tag="u1_1", align_bytes=64)
        nc.vector.tensor_copy(
            out=wbs_dealt[:], in_=wbs_raw[:].rearrange("p (m t) -> p t m", t=PACK)
        )

        ha = [tile([P, J], F32, f"ha{t}") for t in range(PACK)]
        pg = [tile([P, C], F32, f"pg{t}") for t in range(PACK)]
        hid_planes = tile([P, PACK, O], BF16, "hid_planes")
        for t in (0, 1):
            nc.scalar.activation(ha[t][:], acc[t][:], ACT.Relu)
        for t in (3, 2):
            nc.vector.tensor_scalar(ha[t][:], acc[t][:], 0.0, None, ALU.max)
        for t in (0, 1, 2):
            nc.scalar.activation(page[t][:].indirect(list3[:]), ha[t][:], ACT.Copy)
        nc.vector.tensor_copy(page[3][:].indirect(list3[:]), ha[3][:])
        for t in (0, 3, 1, 2):
            nc.vector.tensor_tensor(pg[t][:], page[t][:], old[t][:], ALU.add)
        for t in (0, 3, 1):
            nc.scalar.activation(hid_planes[:, t, :], pg[t][:].indirect(list4[:]), ACT.Copy)
        nc.scalar.activation(hid_planes[:, 2, cols[1]], pg[2][:].indirect(list4[:, halves[1]]), ACT.Copy)
        nc.vector.tensor_copy(hid_planes[:, 2, cols[0]], pg[2][:].indirect(list4[:, halves[0]]))

        hid = [tile([P, HALF, PACK], BF16, f"hid{h}") for h in range(2)]
        hid_codes = tile([P, O], U32, "hid_codes")
        hid_scales = tile([P, O], U8, "hid_scales")
        for h in range(2):
            interleave(nc, hid[h][:], hid_planes[:, :, cols[h]])
        for h in range(2):
            quantize(hid_codes[:, cols[h]], hid_scales[:, cols[h]], hid[h][:], E5M2X4)

        pb = tile([P, PACK, O], F32, "pb")
        squares = tile([P, PACK, O], F32, "squares")
        total = tile([P, PACK], F32, "total")
        sumsq = tile([P, PACK], F32, "sumsq")
        mean = tile([P, PACK], F32, "mean")
        inv = tile([P, PACK], F32, "inv")
        y_low = tile([P, 2, O], F32, "y_low")
        y_high = tile([P, 2, O], F32, "y_high")
        y_rows = out_0.rearrange("(p t) o -> p t o", t=PACK)

        def add_residual(t):
            prod = psum.tile([P, O], F32, name=f"prod{t}")
            nc.tensor.matmul_mx(
                out=prod[:],
                lhsT=wb_dealt[:, t, :].bitcast(E2M1X4),
                lhsT_scale=wbs_dealt[:, t, :],
                rhs=hid_codes[:].bitcast(E5M2X4),
                rhs_scale=hid_scales[:],
                start=True,
                stop=True,
            )
            nc.vector.scalar_tensor_tensor(
                pb[:, t, :], prod[:], 1.0, rs_sb[:, t, :], ALU.mult, ALU.add, accum_out=total[:, t : t + 1]
            )
            nc.scalar.activation(
                squares[:, t, :], pb[:, t, :], ACT.Square, bias=total[:, t : t + 1], scale=-float(O),
                accum_out=sumsq[:, t : t + 1],
            )

        def inverse_spread(pair):
            nc.scalar.activation(inv[:, pair], sumsq[:, pair], ACT.Abs_reciprocal_sqrt, bias=EPS, scale=1.0 / O**3)

        def row_mean(pair):
            nc.vector.tensor_scalar(mean[:, pair], total[:, pair], 1.0 / O, None, ALU.mult)

        def normalise(t, part):
            dst = y_low if t < 2 else y_high
            nc.vector.tensor_scalar(
                dst[:, t % 2, part], pb[:, t, part], mean[:, t : t + 1], inv[:, t : t + 1], ALU.subtract, ALU.mult
            )

        y_bf = [tile([P, HALF, PACK], BF16, f"y_bf{h}") for h in range(2)]
        low, high = slice(0, 2), slice(2, 4)
        add_residual(0)
        add_residual(1)
        add_residual(2)
        inverse_spread(low)
        row_mean(low)
        add_residual(3)
        inverse_spread(slice(2, 3))
        inverse_spread(slice(3, 4))
        normalise(0, slice(0, O))
        row_mean(high)
        normalise(1, slice(0, O))
        nc.sync.dma_start(out=y_rows[:, low, :], in_=y_low[:])
        for h in range(2):
            interleave(nc, y_bf[h][:, :, low], y_low[:, :, cols[h]])
        normalise(2, slice(0, O))
        normalise(3, cols[0])
        normalise(3, cols[1])
        nc.sync.dma_start(out=y_rows[:, high, :], in_=y_high[:])
        y_codes = tile([P, O], U32, "y_codes")
        y_scales = tile([P, O], U8, "y_scales")
        for h in range(2):
            interleave(nc, y_bf[h][:, :, high], y_high[:, :, cols[h]])
        for h in range(2):
            quantize(y_codes[:, cols[h]], y_scales[:, cols[h]], y_bf[h][:], E4M3X4)
        word_rows = out_1[0].rearrange("p c t -> p (c t)").bitcast(I32)
        nc.sync.dma_start(out=word_rows[:, cols[0]], in_=y_codes[:, cols[0]].bitcast(I32))
        nc.scalar.dma_start(out=word_rows[:, cols[1]], in_=y_codes[:, cols[1]].bitcast(I32))
        scale_rows = out_2[0].bitcast(I32)
        for q in range(4):
            queue = nc.scalar if q == 3 else nc.sync
            queue.dma_start(out=scale_rows[4 * q : 4 * q + 4], in_=y_scales[32 * q : 32 * q + 4].bitcast(I32))
